import numpy as np, ml_dtypes
CORES = [2,3,42,43,82,83,122,123]
N = 8
import mx_ref
BF = ml_dtypes.bfloat16
def entries(a):
    return np.ascontiguousarray(a.T).reshape(-1)
def table(e):
    return np.ascontiguousarray(np.reshape(e, (-1, 16)).T).astype(np.int32)
def cols(t, e):
    v = np.concatenate([t.reshape(128, -1, 4), np.zeros((128, 1, 4), BF)], axis=1)
    return np.ascontiguousarray(v[:, e]).reshape(128, -1)
def f(rng, *shape):
    return mx_ref.flush((rng.standard_normal(shape, dtype=np.float32) * np.exp2(rng.integers(-2, 3, shape[:-1] + (1,)))).astype(BF))
def wide(rng, *shape, cols=0):
    v = rng.standard_normal(shape, dtype=np.float32) * np.exp2(rng.integers(-12, 13, shape)).astype(np.float32)
    if cols: v *= np.repeat(np.exp2(rng.integers(-cols, cols + 1, shape[:-2] + (1, shape[-1] // 4))) * (rng.random(shape[:-2] + (1, shape[-1] // 4)) > 0.0625), 4, axis=-1).astype(np.float32)
    return mx_ref.flush(v.astype(BF))
T, NA, S, CAPP = 512, 256, 512, 96
def lists(rng, most=0, inorder=False, big=None):
    c, m = [], []
    for r in range(N):
        n = np.zeros(N, int)
        n[rng.permutation(N)[:most]] = CAPP
        while n.sum() < S:
            q = rng.integers(0, N)
            if n[q] < CAPP: n[q] += 1
        used = np.concatenate([q * CAPP + rng.permutation(CAPP)[:n[q]] for q in range(N)])
        slots = np.full(N * CAPP, -1); slots[used] = rng.integers(0, T, S)
        o = np.sort(used) if inorder else rng.permutation(used)
        if big is not None:
            for i in range(S // 32):
                k = o[32 * i + rng.integers(0, 32)]; slots[k] = rng.choice(big[k // CAPP])
        c.append(table(slots)); m.append(table(o))
    return {"want": np.stack(c), "slot": np.stack(m)}
def setup_inputs(rng):
    return {"v": f(rng, N, 128, 4 * T), "a": f(rng, N, 128, 4 * NA), **lists(rng)}
def setup_inputs_full(rng):
    return {**setup_inputs(rng), **lists(rng, most=S // CAPP)}
def setup_inputs_sorted(rng):
    return {**setup_inputs(rng), **lists(rng, inorder=True)}
def setup_inputs_giant(rng):
    d = setup_inputs(rng); big = [rng.permutation(T)[:T // 32] for q in range(N)]
    x = d["v"].reshape(N, 128, T, 4)
    for q in range(N): x[q][:, big[q]] = (x[q][:, big[q]].astype(np.float32) * np.float32(2.0 ** 20)).astype(BF)
    d["v"] = x.reshape(N, 128, 4 * T)
    return {**d, **lists(rng, big=big)}
def setup_inputs_spread(rng):
    d = setup_inputs(rng); d["v"] = wide(rng, N, 128, 4 * T); d["a"] = wide(rng, N, 128, 4 * NA); return d
def check_inputs(d):
    b = []
    for r in range(N):
        c, m = entries(d["want"][r]), entries(d["slot"][r])
        if c.min() < -1 or c.max() >= T or (c >= 0).sum() != S: b.append("want")
        if m.min() < 0 or m.max() >= N * CAPP or len(set(m.tolist())) != S or (c[np.clip(m, 0, N * CAPP - 1)] < 0).any(): b.append("slot")
    return b
def ones(b):
    e = np.zeros((128, 128, 4), np.float32); e[np.arange(128), np.arange(128), b] = 1
    return e.reshape(128, 512).astype(BF)
def decode(q):
    return np.stack([mx_ref.matmul(mx_ref.quantize(ones(b)), q) for b in range(4)], axis=1).reshape(512, -1)
def reference(v, a, want, slot, own=None):
    h = np.zeros((N, 128, 2048), BF); y = np.zeros((N, 128, 4 * NA), np.float32)
    for r in range(N):
        c = entries(want[r])
        arrived = np.concatenate([decode(mx_ref.quantize(cols(v[q], c[q * CAPP:(q + 1) * CAPP]))) for q in range(N)], axis=1)
        H = arrived[:, entries(slot[r])].T
        h[r] = H.reshape(128, 4, 512).transpose(0, 2, 1).reshape(128, 2048).astype(BF)
    for r in range(N):
        t = h[r] if own is None else np.asarray(own["h"][r])
        for o in range(4):
            y[r][:, NA * o:NA * o + NA] = mx_ref.matmul(mx_ref.quantize(np.ascontiguousarray(t[:, 512 * o:512 * o + 512])), mx_ref.quantize(a[r]))
    return {"y": y, "h": h}

@@ -1,0 +1,296 @@
+from concourse.bass import DstId, RemoteDMATransfer
+from concourse.mybir import dt, AluOpType, ActivationFunctionType
+
+N, CAPP, NV, NA, S = 8, 96, 512, 256, 512
+W = N * CAPP
+LW = CAPP // 16
+COPY = ActivationFunctionType.Copy
+
+SCRATCH = {
+    "w32": ("sbuf", [128, N * LW], "int32"),
+    "w16": ("sbuf", [128, N * LW], "uint16"),
+    "lst": ("sbuf", [128, N * LW], "uint16"),
+    "s32": ("sbuf", [128, S // 16], "int32"),
+    "s16": ("sbuf", [128, S // 16], "uint16"),
+    "vt": ("sbuf", [128, 4 * NV], "bfloat16"),
+    "at": ("sbuf", [128, 4 * NA], "bfloat16"),
+    "aq": ("sbuf", [128, NA], "float8_e4m3fn_x4"),
+    "ap": ("sbuf", [128, NA], "uint8"),
+    "mi": ("sbuf", [128, 128], "float32"),
+    "pi": ("sbuf", [128, 4], "float32"),
+    "jt": ("sbuf", [128, 512], "bfloat16"),
+    "et": ("sbuf", [128, 2048], "bfloat16"),
+    "eq": ("sbuf", [128, 512], "float8_e4m3fn_x4"),
+    "ep": ("sbuf", [128, 512], "uint8"),
+    "ident": ("sbuf", [128, 128], "float32"),
+    "x0": ("sbuf", [128, 512], "bfloat16"),
+    "x1": ("sbuf", [128, 4 * 384], "bfloat16"),
+    "x2": ("sbuf", [128, 4 * 288], "bfloat16"),
+    "q0": ("sbuf", [128, 128], "float8_e4m3fn_x4"),
+    "p0": ("sbuf", [128, 128], "uint8"),
+    "q1": ("sbuf", [128, 384], "float8_e4m3fn_x4"),
+    "p1": ("sbuf", [128, 384], "uint8"),
+    "q2": ("sbuf", [128, 288], "float8_e4m3fn_x4"),
+    "p2": ("sbuf", [128, 288], "uint8"),
+    "cq": ("sbuf", [128, W], "float8_e4m3fn_x4"),
+    "cp": ("sbuf", [128, W], "uint8"),
+    "dw": ("sbuf", [128, 4 * W], "bfloat16"),
+    "gt": ("sbuf", [128, 4 * S], "float32"),
+    "ht": ("sbuf", [128, 4 * S], "bfloat16"),
+    "hq": ("sbuf", [128, S], "float8_e4m3fn_x4"),
+    "hp": ("sbuf", [128, S], "uint8"),
+    "yt": ("sbuf", [128, 4 * NA], "float32"),
+    "psu": ("psum", [128, 2048], "float32"),
+    "pst": ("psum", [128, 1024], "float32"),
+    "psy": ("psum", [128, 1024], "float32"),
+}
+NEV = 80
+SEMAPHORES = (["lst1", "lst2", "loc"] + ["arr%d" % k for k in range(N // 2)] + ["dw%d" % k for k in range(4)]
+              + ["e%d" % k for k in range(NEV)])
+
+
+def relation(topo, a, b):
+    ca, cb = topo.chip(a), topo.chip(b)
+    return 2 if ca == cb else 1 if topo.same_plane(ca, cb) else 0
+
+
+def peers(topo, cores, r):
+    return sorted([q for q in range(N) if q != r], key=lambda q: (relation(topo, cores[r], cores[q]), q))
+
+
+def groups(topo, cores, r):
+    o = peers(topo, cores, r)
+    far = [q for q in o if relation(topo, cores[r], cores[q]) == 0]
+    return far, [q for q in o if q not in far]
+
+
+def lanes(topo, cores, r, group):
+    off = [q for q in group if relation(topo, cores[r], cores[q]) < 2]
+    eng = topo.engines(cores[r], cores[off[0]])
+    wide = 1
+    while 2 * wide * len(off) <= len(eng):
+        wide *= 2
+    spare = (len(eng) - wide * len(off)) // wide
+    out, at = {}, 0
+    for k, q in enumerate(off):
+        n = 2 * wide if len(off) - k <= spare else wide
+        out[q] = eng[at:at + n]
+        at += n
+    for q in group:
+        if q not in out:
+            out[q] = [e for e in topo.engines(cores[r], cores[q]) if e not in eng][:2]
+    return out
+
+
+def rank_program(g, core, T, topo):
+    r = T.rank_of(core)
+    if r is None:
+        return
+    cores = list(T.cores)
+    V, A, P, Y = g.vector, g.scalar, g.tensor, g.sync
+    order = peers(topo, cores, r)
+    rel = {q: relation(topo, cores[r], cores[q]) for q in order}
+    group1, group2 = groups(topo, cores, r)
+    used, nloc = [0], [0]
+
+    def ev():
+        used[0] += 1
+        return T.sem["e%d" % (used[0] - 1)]
+
+    def send(group, piece, sem_of):
+        eng = lanes(topo, cores, r, group)
+        tr = []
+        for q in group:
+            rid, pid, _ = topo.addr(cores[q])
+            src, dst = piece(q)
+            m = 0
+            for e in eng[q]:
+                m += 1 << e
+            tr.append(RemoteDMATransfer(dst_ids=[DstId(rid=rid, pnc=pid)], dma_engine_mask=m, remote_sem=sem_of(q),
+                                        src=src, dst=dst))
+            nloc[0] += len(eng[q])
+        g.remote_dma_fused(tr, local_sem=T.sem.loc)
+
+    e_w, e_v, e_s, e_a = ev(), ev(), ev(), ev()
+    for k in range(8):
+        (Y if k % 2 == 0 else A).dma_start(T.w32[16 * k:16 * k + 16, :], T.want[:]).then_inc(e_w, 16)
+    Y.dma_start(T.vt[:], T.v[:]).then_inc(e_v, 16)
+    for k in range(8):
+        Y.dma_start(T.s32[16 * k:16 * k + 16, :], T.slot[:]).then_inc(e_s, 16)
+    Y.dma_start(T.at[:], T.a[:]).then_inc(e_a, 16)
+
+    e_i, e_z, e_j = ev(), ev(), ev()
+    g.iota(T.mi[:], [[1, 128]], 0, 0, allow_small_or_imprecise_dtypes=True).then_inc(e_i, 1)
+    g.iota(T.pi[:], [[-128, 4]], 0, 4, allow_small_or_imprecise_dtypes=True).then_inc(e_i, 1)
+    V.memset(T.x0[:, 4 * CAPP:512], 0.0).then_inc(e_z, 1)
+    V.wait_ge(e_i, 2)
+    for t in range(4):
+        V.tensor_scalar(T.jt[:, t:512:4], T.mi[:], float(t), None, AluOpType.subtract).then_inc(e_j, 1)
+
+    e_c = ev()
+    V.wait_ge(e_w, 128)
+    V.tensor_scalar(T.w16[:], T.w32[:], 0.0, 4.0, AluOpType.max, AluOpType.mult).then_inc(e_c, 1)
+
+    def list_piece(q):
+        k = peers(topo, cores, q).index(r)
+        return T.w16[:, LW * q:LW * q + LW], T.lst[:, LW * k:LW * k + LW]
+
+    g.wait_ge(e_c, 1)
+    send(order, list_piece, lambda q: T.sem.lst1 if rel[q] == 0 else T.sem.lst2)
+
+    e_e, e_eq = ev(), ev()
+    V.wait_ge(e_j, 4)
+    for o in range(4):
+        V.tensor_scalar(T.et[:, 512 * o:512 * o + 512], T.jt[:], T.pi[:, o:o + 1], None, AluOpType.is_equal).then_inc(e_e, 1)
+    V.wait_ge(e_e, 4)
+    V.quantize_mx(T.eq[:], T.ep[:], T.et[:]).then_inc(e_eq, 1)
+
+    e_g0, e_q0, e_own = ev(), ev(), ev()
+    A.wait_ge(e_v, 16)
+    A.wait_ge(e_c, 1)
+    for t in range(4):
+        A.activation(T.x0[:, t:4 * CAPP:4], T.vt[:, t:4 * NV].indirect(T.w16[:, LW * r:LW * r + LW]), COPY).then_inc(e_g0, 1)
+    V.wait_ge(e_z, 1)
+    V.wait_ge(e_g0, 4)
+    V.quantize_mx(T.q0[:], T.p0[:], T.x0[:]).then_inc(e_q0, 1)
+    Y.wait_ge(e_q0, 1)
+    Y.dma_start(T.cq[:, CAPP * r:CAPP * r + CAPP].bitcast(dt.uint8), T.q0[:, 0:CAPP].bitcast(dt.uint8)).then_inc(e_own, 16)
+    Y.dma_start(T.cp[:, CAPP * r:CAPP * r + CAPP], T.p0[:, 0:CAPP]).then_inc(e_own, 16)
+
+    V.wait_ge(e_v, 16)
+    c0 = 0
+    for grp, lsem, x, qb, pb in ((group1, T.sem.lst1, T.x1, T.q1, T.p1), (group2, T.sem.lst2, T.x2, T.q2, T.p2)):
+        need = sum(len(lanes(topo, cores, s, peers(topo, cores, s))[r]) for s in grp)
+        n = CAPP * len(grp)
+        off = T.lst[:, LW * c0:LW * (c0 + len(grp))]
+        e_g, e_q = ev(), ev()
+        V.wait_ge(lsem, need)
+        A.wait_ge(lsem, need)
+        for t in range(4):
+            win = T.vt[:, t:4 * NV].indirect(off)
+            if t % 2 == 0:
+                V.tensor_copy(x[:, t:4 * n:4], win).then_inc(e_g, 1)
+            else:
+                A.activation(x[:, t:4 * n:4], win, COPY).then_inc(e_g, 1)
+        V.wait_ge(e_g, 4)
+        V.quantize_mx(qb[:], pb[:], x[:]).then_inc(e_q, 1)
+        g.wait_ge(e_q, 1)
+
+        def codes(q):
+            k = CAPP * grp.index(q)
+            return qb[:, k:k + CAPP].bitcast(dt.uint8), T.cq[:, CAPP * r:CAPP * r + CAPP].bitcast(dt.uint8)
+
+        def planes(q):
+            k = CAPP * grp.index(q)
+            return pb[:, k:k + CAPP], T.cp[:, CAPP * r:CAPP * r + CAPP]
+
+        send(grp, codes, lambda q: T.sem["arr%d" % (r // 2)])
+        send(grp, planes, lambda q: T.sem["arr%d" % (r // 2)])
+        c0 += len(grp)
+    g.wait_ge(T.sem.loc, nloc[0])
+
+    e_id, e_s16, e_aq = ev(), ev(), ev()
+    V.tensor_scalar(T.ident[:], T.mi[:], 4.0, T.pi[:, 0:1], AluOpType.mult, AluOpType.is_equal).then_inc(e_id, 1)
+    V.wait_ge(e_s, 128)
+    V.tensor_copy(T.s16[:], T.s32[:]).then_inc(e_s16, 1)
+    V.wait_ge(e_a, 16)
+    V.quantize_mx(T.aq[:], T.ap[:], T.at[:]).then_inc(e_aq, 1)
+
+    PW = 2 * CAPP
+    pairs = [r // 2]
+    for q in order:
+        if q // 2 not in pairs:
+            pairs.append(q // 2)
+    P.wait_ge(e_eq, 1)
+    for c, k in enumerate(pairs):
+        need = 0
+        for s in (2 * k, 2 * k + 1):
+            if s != r:
+                grp = [x for x in groups(topo, cores, s) if r in x][0]
+                need += 2 * len(lanes(topo, cores, s, grp)[r])
+        if c == 0:
+            P.wait_ge(e_own, 32)
+        P.wait_ge(T.sem["arr%d" % k], need)
+        for o in range(4):
+            e_u, e_d = ev(), T.sem["dw%d" % o]
+            if c:
+                P.wait_ge(e_d, c)
+            P.matmul_mx(T.psu[:, 512 * o:512 * o + PW], T.eq[:, 128 * o:128 * o + 128], T.ep[:, 128 * o:128 * o + 128],
+                        T.cq[:, PW * k:PW * k + PW], T.cp[:, PW * k:PW * k + PW], True, True).then_inc(e_u, 1)
+            out, src = T.dw[:, W * o + PW * k:W * o + PW * k + PW], T.psu[:, 512 * o:512 * o + PW]
+            if o % 2 == 0:
+                V.wait_ge(e_u, 1)
+                V.tensor_copy(out, src).then_inc(e_d, 1)
+            else:
+                A.wait_ge(e_u, 1)
+                A.activation(out, src, COPY).then_inc(e_d, 1)
+
+    e_gt = [ev() for _ in range(4)]
+    V.wait_ge(e_s16, 1)
+    A.wait_ge(e_s16, 1)
+    hs = S // 2
+    for o in range(4):
+        win = T.dw[:, W * o:W * o + W]
+        V.wait_ge(T.sem["dw%d" % o], 4)
+        V.tensor_copy(T.gt[:, S * o:S * o + hs], win.indirect(T.s16[:, 0:hs // 16])).then_inc(e_gt[o], 1)
+        A.wait_ge(T.sem["dw%d" % o], 4)
+        A.activation(T.gt[:, S * o + hs:S * o + S], win.indirect(T.s16[:, hs // 16:S // 16]), COPY).then_inc(e_gt[o], 1)
+
+    e_t, e_h, e_hq, e_y, e_ye = ([ev() for _ in range(4)] for _ in range(5))
+    e_out = ev()
+
+    def turn(o):
+        P.wait_ge(e_gt[o], 2)
+        if o >= 2:
+            P.wait_ge(e_h[o - 2], 1)
+        b = 512 * (o % 2)
+        for t in range(4):
+            P.transpose(T.pst[:, b + t:b + 512:4], T.gt[:, S * o + t:S * o + S:4], T.ident[:]).then_inc(e_t[o], 1)
+
+    def product(o):
+        P.wait_ge(e_hq[o], 1)
+        if o >= 2:
+            P.wait_ge(e_ye[o - 2], 1)
+        b = 512 * (o % 2)
+        P.matmul_mx(T.psy[:, b:b + NA], T.hq[:, 128 * o:128 * o + 128], T.hp[:, 128 * o:128 * o + 128], T.aq[:], T.ap[:],
+                    True, True).then_inc(e_y[o], 1)
+
+    P.wait_ge(e_id, 1)
+    turn(0)
+    turn(1)
+    P.wait_ge(e_aq, 1)
+    product(0)
+    turn(2)
+    product(1)
+    turn(3)
+    product(2)
+    product(3)
+
+    def h_out(o):
+        out, src = T.ht[:, 512 * o:512 * o + 512], T.pst[:, 512 * (o % 2):512 * (o % 2) + 512]
+        if o % 2 == 0:
+            A.wait_ge(e_t[o], 4)
+            A.activation(out, src, COPY).then_inc(e_h[o], 1)
+        else:
+            V.wait_ge(e_t[o], 4)
+            V.tensor_copy(out, src).then_inc(e_h[o], 1)
+        V.wait_ge(e_h[o], 1)
+        V.quantize_mx(T.hq[:, 128 * o:128 * o + 128], T.hp[:, 128 * o:128 * o + 128], out).then_inc(e_hq[o], 1)
+        Y.wait_ge(e_h[o], 1)
+        Y.dma_start(T.h[:, 512 * o:512 * o + 512], out).then_inc(e_out, 16)
+
+    def y_out(o):
+        A.wait_ge(e_y[o], 1)
+        A.activation(T.yt[:, NA * o:NA * o + NA], T.psy[:, 512 * (o % 2):512 * (o % 2) + NA], COPY).then_inc(e_ye[o], 1)
+        Y.wait_ge(e_ye[o], 1)
+        Y.dma_start(T.y[:, NA * o:NA * o + NA], T.yt[:, NA * o:NA * o + NA]).then_inc(e_out, 16)
+
+    h_out(0)
+    h_out(1)
+    y_out(0)
+    h_out(2)
+    y_out(1)
+    h_out(3)
+    y_out(2)
+    y_out(3)
+    Y.wait_ge(e_out, 128)

@@ -5,6 +5,9 @@ N, CAPP, NV, NA, S = 8, 96, 512, 256, 512
 W = N * CAPP
 LW = CAPP // 16
 COPY = ActivationFunctionType.Copy
+OWNAT = 1.5
+UORD = [0, 3, 2, 1]
+TAIL = "p0 L p1 t0 t1 e0V q0 m0 y0 e1 l2 q2 m2 q1 m1 y2 y1 l3 q3 m3 y3V"
 
 SCRATCH = {
     "w32": ("sbuf", [128, N * LW], "int32"),
@@ -12,30 +15,28 @@ SCRATCH = {
     "lst": ("sbuf", [128, N * LW], "uint16"),
     "s32": ("sbuf", [128, S // 16], "int32"),
     "s16": ("sbuf", [128, S // 16], "uint16"),
+    "sl": ("sbuf", [128, S // 8], "uint16"),
     "vt": ("sbuf", [128, 4 * NV], "bfloat16"),
     "at": ("sbuf", [128, 4 * NA], "bfloat16"),
     "aq": ("sbuf", [128, NA], "float8_e4m3fn_x4"),
     "ap": ("sbuf", [128, NA], "uint8"),
     "mi": ("sbuf", [128, 128], "float32"),
-    "pi": ("sbuf", [128, 4], "float32"),
+    "pi": ("sbuf", [128, 16], "float32"),
     "jt": ("sbuf", [128, 512], "bfloat16"),
+    "jl": ("sbuf", [128, 512], "bfloat16"),
     "et": ("sbuf", [128, 2048], "bfloat16"),
     "eq": ("sbuf", [128, 512], "float8_e4m3fn_x4"),
     "ep": ("sbuf", [128, 512], "uint8"),
     "ident": ("sbuf", [128, 128], "float32"),
     "x0": ("sbuf", [128, 512], "bfloat16"),
-    "x1": ("sbuf", [128, 4 * 384], "bfloat16"),
-    "x2": ("sbuf", [128, 4 * 288], "bfloat16"),
     "q0": ("sbuf", [128, 128], "float8_e4m3fn_x4"),
     "p0": ("sbuf", [128, 128], "uint8"),
-    "q1": ("sbuf", [128, 384], "float8_e4m3fn_x4"),
-    "p1": ("sbuf", [128, 384], "uint8"),
-    "q2": ("sbuf", [128, 288], "float8_e4m3fn_x4"),
-    "p2": ("sbuf", [128, 288], "uint8"),
     "cq": ("sbuf", [128, W], "float8_e4m3fn_x4"),
     "cp": ("sbuf", [128, W], "uint8"),
     "dw": ("sbuf", [128, 4 * W], "bfloat16"),
-    "gt": ("sbuf", [128, 4 * S], "float32"),
+    "gt": ("sbuf", [128, 2 * S], "float32"),
+    "gl": ("sbuf", [128, 2 * S], "bfloat16"),
+    "gm": ("sbuf", [128, 2 * S], "bfloat16"),
     "ht": ("sbuf", [128, 4 * S], "bfloat16"),
     "hq": ("sbuf", [128, S], "float8_e4m3fn_x4"),
     "hp": ("sbuf", [128, S], "uint8"),
@@ -44,8 +45,12 @@ SCRATCH = {
     "pst": ("psum", [128, 1024], "float32"),
     "psy": ("psum", [128, 1024], "float32"),
 }
-NEV = 80
-SEMAPHORES = (["lst1", "lst2", "loc"] + ["arr%d" % k for k in range(N // 2)] + ["dw%d" % k for k in range(4)]
+for _k, _n in ((1, 2), (2, 3), (3, 2)):
+    SCRATCH["x%d" % _k] = ("sbuf", [128, 4 * CAPP * _n], "bfloat16")
+    SCRATCH["q%d" % _k] = ("sbuf", [128, CAPP * _n], "float8_e4m3fn_x4")
+    SCRATCH["p%d" % _k] = ("sbuf", [128, CAPP * _n], "uint8")
+NEV = 96
+SEMAPHORES = (["lst1", "lst2", "lst3", "loc"] + ["arr%d" % k for k in range(N // 2)] + ["dw%d" % k for k in range(4)]
               + ["e%d" % k for k in range(NEV)])
 
 
@@ -54,14 +59,15 @@ def relation(topo, a, b):
     return 2 if ca == cb else 1 if topo.same_plane(ca, cb) else 0
 
 
+def batches(topo, cores, r):
+    rel = [relation(topo, cores[r], c) for c in cores]
+    near = sorted([q for q in range(N) if q != r], key=lambda q: (q // 2 - r // 2) % (N // 2) * N + q)
+    far = [q for q in near if rel[q] == 0]
+    return [far[:2], far[2:] + [q for q in near if rel[q] == 2], [q for q in near if rel[q] == 1]]
+
+
 def peers(topo, cores, r):
-    return sorted([q for q in range(N) if q != r], key=lambda q: (relation(topo, cores[r], cores[q]), q))
-
-
-def groups(topo, cores, r):
-    o = peers(topo, cores, r)
-    far = [q for q in o if relation(topo, cores[r], cores[q]) == 0]
-    return far, [q for q in o if q not in far]
+    return [q for b in batches(topo, cores, r) for q in b]
 
 
 def lanes(topo, cores, r, group):
@@ -89,13 +95,17 @@ def rank_program(g, core, T, topo):
     cores = list(T.cores)
     V, A, P, Y = g.vector, g.scalar, g.tensor, g.sync
     order = peers(topo, cores, r)
-    rel = {q: relation(topo, cores[r], cores[q]) for q in order}
-    group1, group2 = groups(topo, cores, r)
     used, nloc = [0], [0]
 
     def ev():
         used[0] += 1
         return T.sem["e%d" % (used[0] - 1)]
+
+    def copy(q, out, src, sem):
+        if q is V:
+            V.tensor_copy(out, src).then_inc(sem, 1)
+        else:
+            A.activation(out, src, COPY).then_inc(sem, 1)
 
     def send(group, piece, sem_of):
         eng = lanes(topo, cores, r, group)
@@ -111,6 +121,9 @@ def rank_program(g, core, T, topo):
             nloc[0] += len(eng[q])
         g.remote_dma_fused(tr, local_sem=T.sem.loc)
 
+    def batch_of(s, q):
+        return [q in b for b in batches(topo, cores, s)].index(True)
+
     e_w, e_v, e_s, e_a = ev(), ev(), ev(), ev()
     for k in range(8):
         (Y if k % 2 == 0 else A).dma_start(T.w32[16 * k:16 * k + 16, :], T.want[:]).then_inc(e_w, 16)
@@ -119,9 +132,9 @@ def rank_program(g, core, T, topo):
         Y.dma_start(T.s32[16 * k:16 * k + 16, :], T.slot[:]).then_inc(e_s, 16)
     Y.dma_start(T.at[:], T.a[:]).then_inc(e_a, 16)
 
-    e_i, e_z, e_j = ev(), ev(), ev()
+    e_i, e_z, e_j, e_k = ev(), ev(), ev(), ev()
     g.iota(T.mi[:], [[1, 128]], 0, 0, allow_small_or_imprecise_dtypes=True).then_inc(e_i, 1)
-    g.iota(T.pi[:], [[-128, 4]], 0, 4, allow_small_or_imprecise_dtypes=True).then_inc(e_i, 1)
+    g.iota(T.pi[:], [[-32, 16]], 0, 4, allow_small_or_imprecise_dtypes=True).then_inc(e_i, 1)
     V.memset(T.x0[:, 4 * CAPP:512], 0.0).then_inc(e_z, 1)
     V.wait_ge(e_i, 2)
     for t in range(4):
@@ -136,12 +149,20 @@ def rank_program(g, core, T, topo):
         return T.w16[:, LW * q:LW * q + LW], T.lst[:, LW * k:LW * k + LW]
 
     g.wait_ge(e_c, 1)
-    send(order, list_piece, lambda q: T.sem.lst1 if rel[q] == 0 else T.sem.lst2)
+    send(order, list_piece, lambda q: T.sem["lst%d" % (1 + batch_of(q, r))])
 
     e_e, e_eq = ev(), ev()
     V.wait_ge(e_j, 4)
-    for o in range(4):
-        V.tensor_scalar(T.et[:, 512 * o:512 * o + 512], T.jt[:], T.pi[:, o:o + 1], None, AluOpType.is_equal).then_inc(e_e, 1)
+    for s in range(4):
+        V.tensor_scalar(T.jl[:, 128 * s:128 * s + 128], T.jt[:, 128 * s:128 * s + 128], 32.0 * s, None,
+                        AluOpType.add).then_inc(e_k, 1)
+    for o in range(2):
+        V.tensor_scalar(T.et[:, 512 * o:512 * o + 512], T.jt[:], T.pi[:, 4 * o:4 * o + 1], None,
+                        AluOpType.is_equal).then_inc(e_e, 1)
+    V.wait_ge(e_k, 4)
+    for b in range(2):
+        V.tensor_scalar(T.et[:, 1024 + 512 * b:1536 + 512 * b], T.jl[:], T.pi[:, 8 + b:9 + b], None,
+                        AluOpType.is_equal).then_inc(e_e, 1)
     V.wait_ge(e_e, 4)
     V.quantize_mx(T.eq[:], T.ep[:], T.et[:]).then_inc(e_eq, 1)
 
@@ -159,19 +180,16 @@ def rank_program(g, core, T, topo):
 
     V.wait_ge(e_v, 16)
     c0 = 0
-    for grp, lsem, x, qb, pb in ((group1, T.sem.lst1, T.x1, T.q1, T.p1), (group2, T.sem.lst2, T.x2, T.q2, T.p2)):
+    for i, grp in enumerate(batches(topo, cores, r)):
+        x, qb, pb = T["x%d" % (i + 1)], T["q%d" % (i + 1)], T["p%d" % (i + 1)]
         need = sum(len(lanes(topo, cores, s, peers(topo, cores, s))[r]) for s in grp)
         n = CAPP * len(grp)
         off = T.lst[:, LW * c0:LW * (c0 + len(grp))]
         e_g, e_q = ev(), ev()
-        V.wait_ge(lsem, need)
-        A.wait_ge(lsem, need)
+        V.wait_ge(T.sem["lst%d" % (i + 1)], need)
+        A.wait_ge(T.sem["lst%d" % (i + 1)], need)
         for t in range(4):
-            win = T.vt[:, t:4 * NV].indirect(off)
-            if t % 2 == 0:
-                V.tensor_copy(x[:, t:4 * n:4], win).then_inc(e_g, 1)
-            else:
-                A.activation(x[:, t:4 * n:4], win, COPY).then_inc(e_g, 1)
+            copy(V if t % 2 == 0 else A, x[:, t:4 * n:4], T.vt[:, t:4 * NV].indirect(off), e_g)
         V.wait_ge(e_g, 4)
         V.quantize_mx(qb[:], pb[:], x[:]).then_inc(e_q, 1)
         g.wait_ge(e_q, 1)
@@ -189,108 +207,115 @@ def rank_program(g, core, T, topo):
         c0 += len(grp)
     g.wait_ge(T.sem.loc, nloc[0])
 
-    e_id, e_s16, e_aq = ev(), ev(), ev()
+    e_id, e_s16, e_sl, e_aq = ev(), ev(), ev(), ev()
     V.tensor_scalar(T.ident[:], T.mi[:], 4.0, T.pi[:, 0:1], AluOpType.mult, AluOpType.is_equal).then_inc(e_id, 1)
     V.wait_ge(e_s, 128)
     V.tensor_copy(T.s16[:], T.s32[:]).then_inc(e_s16, 1)
+    for a in range(4):
+        for b in range(2):
+            V.tensor_scalar(T.sl[:, 16 * a + 8 * b:16 * a + 8 * b + 8], T.s32[:, 8 * a:8 * a + 8], float(b * W), None,
+                            AluOpType.add).then_inc(e_sl, 1)
     V.wait_ge(e_a, 16)
     V.quantize_mx(T.aq[:], T.ap[:], T.at[:]).then_inc(e_aq, 1)
 
     PW = 2 * CAPP
-    pairs = [r // 2]
-    for q in order:
-        if q // 2 not in pairs:
-            pairs.append(q // 2)
+    pairs = sorted(range(N // 2), key=lambda k: OWNAT if k == r // 2 else batch_of(2 * k, r))
     P.wait_ge(e_eq, 1)
     for c, k in enumerate(pairs):
         need = 0
         for s in (2 * k, 2 * k + 1):
             if s != r:
-                grp = [x for x in groups(topo, cores, s) if r in x][0]
-                need += 2 * len(lanes(topo, cores, s, grp)[r])
-        if c == 0:
+                need += 2 * len(lanes(topo, cores, s, batches(topo, cores, s)[batch_of(s, r)])[r])
+        if k == r // 2:
             P.wait_ge(e_own, 32)
         P.wait_ge(T.sem["arr%d" % k], need)
-        for o in range(4):
+        for o in UORD:
             e_u, e_d = ev(), T.sem["dw%d" % o]
             if c:
                 P.wait_ge(e_d, c)
             P.matmul_mx(T.psu[:, 512 * o:512 * o + PW], T.eq[:, 128 * o:128 * o + 128], T.ep[:, 128 * o:128 * o + 128],
                         T.cq[:, PW * k:PW * k + PW], T.cp[:, PW * k:PW * k + PW], True, True).then_inc(e_u, 1)
-            out, src = T.dw[:, W * o + PW * k:W * o + PW * k + PW], T.psu[:, 512 * o:512 * o + PW]
-            if o % 2 == 0:
-                V.wait_ge(e_u, 1)
-                V.tensor_copy(out, src).then_inc(e_d, 1)
-            else:
-                A.wait_ge(e_u, 1)
-                A.activation(out, src, COPY).then_inc(e_d, 1)
+            q = V if o % 2 == 0 else A
+            q.wait_ge(e_u, 1)
+            copy(q, T.dw[:, W * o + PW * k:W * o + PW * k + PW], T.psu[:, 512 * o:512 * o + PW], e_d)
 
-    e_gt = [ev() for _ in range(4)]
-    V.wait_ge(e_s16, 1)
-    A.wait_ge(e_s16, 1)
-    hs = S // 2
-    for o in range(4):
-        win = T.dw[:, W * o:W * o + W]
-        V.wait_ge(T.sem["dw%d" % o], 4)
-        V.tensor_copy(T.gt[:, S * o:S * o + hs], win.indirect(T.s16[:, 0:hs // 16])).then_inc(e_gt[o], 1)
-        A.wait_ge(T.sem["dw%d" % o], 4)
-        A.activation(T.gt[:, S * o + hs:S * o + S], win.indirect(T.s16[:, hs // 16:S // 16]), COPY).then_inc(e_gt[o], 1)
-
+    e_gt = [ev() for _ in range(2)]
+    e_gl = [ev() for _ in range(2)]
+    e_gm = [ev() for _ in range(2)]
     e_t, e_h, e_hq, e_y, e_ye = ([ev() for _ in range(4)] for _ in range(5))
     e_out = ev()
+    hs = S // 2
+    for q in (V, A):
+        q.wait_ge(e_s16, 1)
+        q.wait_ge(e_sl, 8)
+
+    def pick(o):
+        for h, q in enumerate((V, A)):
+            q.wait_ge(T.sem["dw%d" % o], 4)
+            copy(q, T.gt[:, S * o + hs * h:S * o + hs * h + hs],
+                 T.dw[:, W * o:W * o + W].indirect(T.s16[:, 16 * h:16 * h + 16]), e_gt[o])
+
+    def pick_both():
+        for h, q in enumerate((V, A)):
+            q.wait_ge(T.sem.dw2, 4)
+            q.wait_ge(T.sem.dw3, 4)
+            copy(q, T.gl[:, S * h:S * h + S], T.dw[:, 2 * W:4 * W].indirect(T.sl[:, 32 * h:32 * h + 32]), e_gl[h])
+        for k in range(2):
+            for h in range(2):
+                if k == 0:
+                    Y.wait_ge(e_gl[h], 1)
+                for a in (2 * h, 2 * h + 1):
+                    for s in (2 * k, 2 * k + 1):
+                        Y.dma_start(T.gm[32 * a:32 * a + 32, hs * s:hs * s + hs],
+                                    T.gl[32 * s:32 * s + 32, hs * a:hs * a + hs]).then_inc(e_gm[k], 16)
 
     def turn(o):
         P.wait_ge(e_gt[o], 2)
-        if o >= 2:
-            P.wait_ge(e_h[o - 2], 1)
-        b = 512 * (o % 2)
+        b = 512 * o
         for t in range(4):
-            P.transpose(T.pst[:, b + t:b + 512:4], T.gt[:, S * o + t:S * o + S:4], T.ident[:]).then_inc(e_t[o], 1)
+            P.transpose(T.pst[:, b + t:b + 512:4], T.gt[:, b + t:b + 512:4], T.ident[:]).then_inc(e_t[o], 1)
+
+    def turn_here(o):
+        V.wait_ge(e_gm[o - 2], 128)
+        b = S * (o - 2)
+        for t in range(4):
+            V.transpose(T.ht[:, 512 * o + t:512 * o + 512:4], T.gm[:, b + t:b + S:4]).then_inc(e_h[o], 1)
+
+    def empty(o, q):
+        q.wait_ge(e_t[o], 4)
+        copy(q, T.ht[:, 512 * o:512 * o + 512], T.pst[:, 512 * o:512 * o + 512], e_h[o])
+
+    def quant(o):
+        n = 1 if o < 2 else 4
+        V.wait_ge(e_h[o], n)
+        V.quantize_mx(T.hq[:, 128 * o:128 * o + 128], T.hp[:, 128 * o:128 * o + 128],
+                      T.ht[:, 512 * o:512 * o + 512]).then_inc(e_hq[o], 1)
+        Y.wait_ge(e_h[o], n)
+        Y.dma_start(T.h[:, 512 * o:512 * o + 512], T.ht[:, 512 * o:512 * o + 512]).then_inc(e_out, 16)
+
+    bank = {}
 
     def product(o):
+        n = len(bank)
+        bank[o] = T.psy[:, 512 * n:512 * n + NA] if n < 2 else T.psu[:, 512 * (n - 2):512 * (n - 2) + NA]
         P.wait_ge(e_hq[o], 1)
-        if o >= 2:
-            P.wait_ge(e_ye[o - 2], 1)
-        b = 512 * (o % 2)
-        P.matmul_mx(T.psy[:, b:b + NA], T.hq[:, 128 * o:128 * o + 128], T.hp[:, 128 * o:128 * o + 128], T.aq[:], T.ap[:],
+        P.matmul_mx(bank[o], T.hq[:, 128 * o:128 * o + 128], T.hp[:, 128 * o:128 * o + 128], T.aq[:], T.ap[:],
                     True, True).then_inc(e_y[o], 1)
 
-    P.wait_ge(e_id, 1)
-    turn(0)
-    turn(1)
-    P.wait_ge(e_aq, 1)
-    product(0)
-    turn(2)
-    product(1)
-    turn(3)
-    product(2)
-    product(3)
-
-    def h_out(o):
-        out, src = T.ht[:, 512 * o:512 * o + 512], T.pst[:, 512 * (o % 2):512 * (o % 2) + 512]
-        if o % 2 == 0:
-            A.wait_ge(e_t[o], 4)
-            A.activation(out, src, COPY).then_inc(e_h[o], 1)
-        else:
-            V.wait_ge(e_t[o], 4)
-            V.tensor_copy(out, src).then_inc(e_h[o], 1)
-        V.wait_ge(e_h[o], 1)
-        V.quantize_mx(T.hq[:, 128 * o:128 * o + 128], T.hp[:, 128 * o:128 * o + 128], out).then_inc(e_hq[o], 1)
-        Y.wait_ge(e_h[o], 1)
-        Y.dma_start(T.h[:, 512 * o:512 * o + 512], out).then_inc(e_out, 16)
-
-    def y_out(o):
-        A.wait_ge(e_y[o], 1)
-        A.activation(T.yt[:, NA * o:NA * o + NA], T.psy[:, 512 * (o % 2):512 * (o % 2) + NA], COPY).then_inc(e_ye[o], 1)
+    def y_out(o, q):
+        q.wait_ge(e_y[o], 1)
+        copy(q, T.yt[:, NA * o:NA * o + NA], bank[o], e_ye[o])
         Y.wait_ge(e_ye[o], 1)
         Y.dma_start(T.y[:, NA * o:NA * o + NA], T.yt[:, NA * o:NA * o + NA]).then_inc(e_out, 16)
 
-    h_out(0)
-    h_out(1)
-    y_out(0)
-    h_out(2)
-    y_out(1)
-    h_out(3)
-    y_out(2)
-    y_out(3)
+    P.wait_ge(e_id, 1)
+    P.wait_ge(e_aq, 1)
+    step = {"p": pick, "t": turn, "l": turn_here, "q": quant, "m": product, "e": empty, "y": y_out}
+    for w in TAIL.split():
+        if w == "L":
+            pick_both()
+        elif w[0] in "ey":
+            step[w[0]](int(w[1]), V if w[2:] == "V" else A)
+        else:
+            step[w[0]](int(w[1]))
     Y.wait_ge(e_out, 128)

from concourse.bass import DstId, RemoteDMATransfer
from concourse.mybir import dt, AluOpType, ActivationFunctionType

N, CAPP, NV, NA, S = 8, 96, 512, 256, 512
W = N * CAPP
LW = CAPP // 16
COPY = ActivationFunctionType.Copy
OWNAT = 1.5
UORD = [0, 3, 2, 1]
TAIL = "p0 L p1 t0 t1 e0V q0 m0 y0 e1 l2 q2 m2 q1 m1 y2 y1 l3 q3 m3 y3V"

SCRATCH = {
    "w32": ("sbuf", [128, N * LW], "int32"),
    "w16": ("sbuf", [128, N * LW], "uint16"),
    "lst": ("sbuf", [128, N * LW], "uint16"),
    "s32": ("sbuf", [128, S // 16], "int32"),
    "s16": ("sbuf", [128, S // 16], "uint16"),
    "sl": ("sbuf", [128, S // 8], "uint16"),
    "vt": ("sbuf", [128, 4 * NV], "bfloat16"),
    "at": ("sbuf", [128, 4 * NA], "bfloat16"),
    "aq": ("sbuf", [128, NA], "float8_e4m3fn_x4"),
    "ap": ("sbuf", [128, NA], "uint8"),
    "mi": ("sbuf", [128, 128], "float32"),
    "pi": ("sbuf", [128, 16], "float32"),
    "jt": ("sbuf", [128, 512], "bfloat16"),
    "jl": ("sbuf", [128, 512], "bfloat16"),
    "et": ("sbuf", [128, 2048], "bfloat16"),
    "eq": ("sbuf", [128, 512], "float8_e4m3fn_x4"),
    "ep": ("sbuf", [128, 512], "uint8"),
    "ident": ("sbuf", [128, 128], "float32"),
    "x0": ("sbuf", [128, 512], "bfloat16"),
    "q0": ("sbuf", [128, 128], "float8_e4m3fn_x4"),
    "p0": ("sbuf", [128, 128], "uint8"),
    "cq": ("sbuf", [128, W], "float8_e4m3fn_x4"),
    "cp": ("sbuf", [128, W], "uint8"),
    "dw": ("sbuf", [128, 4 * W], "bfloat16"),
    "gt": ("sbuf", [128, 2 * S], "float32"),
    "gl": ("sbuf", [128, 2 * S], "bfloat16"),
    "gm": ("sbuf", [128, 2 * S], "bfloat16"),
    "ht": ("sbuf", [128, 4 * S], "bfloat16"),
    "hq": ("sbuf", [128, S], "float8_e4m3fn_x4"),
    "hp": ("sbuf", [128, S], "uint8"),
    "yt": ("sbuf", [128, 4 * NA], "float32"),
    "psu": ("psum", [128, 2048], "float32"),
    "pst": ("psum", [128, 1024], "float32"),
    "psy": ("psum", [128, 1024], "float32"),
}
for _k, _n in ((1, 2), (2, 3), (3, 2)):
    SCRATCH["x%d" % _k] = ("sbuf", [128, 4 * CAPP * _n], "bfloat16")
    SCRATCH["q%d" % _k] = ("sbuf", [128, CAPP * _n], "float8_e4m3fn_x4")
    SCRATCH["p%d" % _k] = ("sbuf", [128, CAPP * _n], "uint8")
NEV = 96
SEMAPHORES = (["lst1", "lst2", "lst3", "loc"] + ["arr%d" % k for k in range(N // 2)] + ["dw%d" % k for k in range(4)]
              + ["e%d" % k for k in range(NEV)])


def relation(topo, a, b):
    ca, cb = topo.chip(a), topo.chip(b)
    return 2 if ca == cb else 1 if topo.same_plane(ca, cb) else 0


def batches(topo, cores, r):
    rel = [relation(topo, cores[r], c) for c in cores]
    near = sorted([q for q in range(N) if q != r], key=lambda q: (q // 2 - r // 2) % (N // 2) * N + q)
    far = [q for q in near if rel[q] == 0]
    return [far[:2], far[2:] + [q for q in near if rel[q] == 2], [q for q in near if rel[q] == 1]]


def peers(topo, cores, r):
    return [q for b in batches(topo, cores, r) for q in b]


def lanes(topo, cores, r, group):
    off = [q for q in group if relation(topo, cores[r], cores[q]) < 2]
    eng = topo.engines(cores[r], cores[off[0]])
    wide = 1
    while 2 * wide * len(off) <= len(eng):
        wide *= 2
    spare = (len(eng) - wide * len(off)) // wide
    out, at = {}, 0
    for k, q in enumerate(off):
        n = 2 * wide if len(off) - k <= spare else wide
        out[q] = eng[at:at + n]
        at += n
    for q in group:
        if q not in out:
            out[q] = [e for e in topo.engines(cores[r], cores[q]) if e not in eng][:2]
    return out


def rank_program(g, core, T, topo):
    r = T.rank_of(core)
    if r is None:
        return
    cores = list(T.cores)
    V, A, P, Y = g.vector, g.scalar, g.tensor, g.sync
    order = peers(topo, cores, r)
    used, nloc = [0], [0]

    def ev():
        used[0] += 1
        return T.sem["e%d" % (used[0] - 1)]

    def copy(q, out, src, sem):
        if q is V:
            V.tensor_copy(out, src).then_inc(sem, 1)
        else:
            A.activation(out, src, COPY).then_inc(sem, 1)

    def send(group, piece, sem_of):
        eng = lanes(topo, cores, r, group)
        tr = []
        for q in group:
            rid, pid, _ = topo.addr(cores[q])
            src, dst = piece(q)
            m = 0
            for e in eng[q]:
                m += 1 << e
            tr.append(RemoteDMATransfer(dst_ids=[DstId(rid=rid, pnc=pid)], dma_engine_mask=m, remote_sem=sem_of(q),
                                        src=src, dst=dst))
            nloc[0] += len(eng[q])
        g.remote_dma_fused(tr, local_sem=T.sem.loc)

    def batch_of(s, q):
        return [q in b for b in batches(topo, cores, s)].index(True)

    e_w, e_v, e_s, e_a = ev(), ev(), ev(), ev()
    for k in range(8):
        (Y if k % 2 == 0 else A).dma_start(T.w32[16 * k:16 * k + 16, :], T.want[:]).then_inc(e_w, 16)
    Y.dma_start(T.vt[:], T.v[:]).then_inc(e_v, 16)
    for k in range(8):
        Y.dma_start(T.s32[16 * k:16 * k + 16, :], T.slot[:]).then_inc(e_s, 16)
    Y.dma_start(T.at[:], T.a[:]).then_inc(e_a, 16)

    e_i, e_z, e_j, e_k = ev(), ev(), ev(), ev()
    g.iota(T.mi[:], [[1, 128]], 0, 0, allow_small_or_imprecise_dtypes=True).then_inc(e_i, 1)
    g.iota(T.pi[:], [[-32, 16]], 0, 4, allow_small_or_imprecise_dtypes=True).then_inc(e_i, 1)
    V.memset(T.x0[:, 4 * CAPP:512], 0.0).then_inc(e_z, 1)
    V.wait_ge(e_i, 2)
    for t in range(4):
        V.tensor_scalar(T.jt[:, t:512:4], T.mi[:], float(t), None, AluOpType.subtract).then_inc(e_j, 1)

    e_c = ev()
    V.wait_ge(e_w, 128)
    V.tensor_scalar(T.w16[:], T.w32[:], 0.0, 4.0, AluOpType.max, AluOpType.mult).then_inc(e_c, 1)

    def list_piece(q):
        k = peers(topo, cores, q).index(r)
        return T.w16[:, LW * q:LW * q + LW], T.lst[:, LW * k:LW * k + LW]

    g.wait_ge(e_c, 1)
    send(order, list_piece, lambda q: T.sem["lst%d" % (1 + batch_of(q, r))])

    e_e, e_eq = ev(), ev()
    V.wait_ge(e_j, 4)
    for s in range(4):
        V.tensor_scalar(T.jl[:, 128 * s:128 * s + 128], T.jt[:, 128 * s:128 * s + 128], 32.0 * s, None,
                        AluOpType.add).then_inc(e_k, 1)
    for o in range(2):
        V.tensor_scalar(T.et[:, 512 * o:512 * o + 512], T.jt[:], T.pi[:, 4 * o:4 * o + 1], None,
                        AluOpType.is_equal).then_inc(e_e, 1)
    V.wait_ge(e_k, 4)
    for b in range(2):
        V.tensor_scalar(T.et[:, 1024 + 512 * b:1536 + 512 * b], T.jl[:], T.pi[:, 8 + b:9 + b], None,
                        AluOpType.is_equal).then_inc(e_e, 1)
    V.wait_ge(e_e, 4)
    V.quantize_mx(T.eq[:], T.ep[:], T.et[:]).then_inc(e_eq, 1)

    e_g0, e_q0, e_own = ev(), ev(), ev()
    A.wait_ge(e_v, 16)
    A.wait_ge(e_c, 1)
    for t in range(4):
        A.activation(T.x0[:, t:4 * CAPP:4], T.vt[:, t:4 * NV].indirect(T.w16[:, LW * r:LW * r + LW]), COPY).then_inc(e_g0, 1)
    V.wait_ge(e_z, 1)
    V.wait_ge(e_g0, 4)
    V.quantize_mx(T.q0[:], T.p0[:], T.x0[:]).then_inc(e_q0, 1)
    Y.wait_ge(e_q0, 1)
    Y.dma_start(T.cq[:, CAPP * r:CAPP * r + CAPP].bitcast(dt.uint8), T.q0[:, 0:CAPP].bitcast(dt.uint8)).then_inc(e_own, 16)
    Y.dma_start(T.cp[:, CAPP * r:CAPP * r + CAPP], T.p0[:, 0:CAPP]).then_inc(e_own, 16)

    V.wait_ge(e_v, 16)
    c0 = 0
    for i, grp in enumerate(batches(topo, cores, r)):
        x, qb, pb = T["x%d" % (i + 1)], T["q%d" % (i + 1)], T["p%d" % (i + 1)]
        need = sum(len(lanes(topo, cores, s, peers(topo, cores, s))[r]) for s in grp)
        n = CAPP * len(grp)
        off = T.lst[:, LW * c0:LW * (c0 + len(grp))]
        e_g, e_q = ev(), ev()
        V.wait_ge(T.sem["lst%d" % (i + 1)], need)
        A.wait_ge(T.sem["lst%d" % (i + 1)], need)
        for t in range(4):
            copy(V if t % 2 == 0 else A, x[:, t:4 * n:4], T.vt[:, t:4 * NV].indirect(off), e_g)
        V.wait_ge(e_g, 4)
        V.quantize_mx(qb[:], pb[:], x[:]).then_inc(e_q, 1)
        g.wait_ge(e_q, 1)

        def codes(q):
            k = CAPP * grp.index(q)
            return qb[:, k:k + CAPP].bitcast(dt.uint8), T.cq[:, CAPP * r:CAPP * r + CAPP].bitcast(dt.uint8)

        def planes(q):
            k = CAPP * grp.index(q)
            return pb[:, k:k + CAPP], T.cp[:, CAPP * r:CAPP * r + CAPP]

        send(grp, codes, lambda q: T.sem["arr%d" % (r // 2)])
        send(grp, planes, lambda q: T.sem["arr%d" % (r // 2)])
        c0 += len(grp)
    g.wait_ge(T.sem.loc, nloc[0])

    e_id, e_s16, e_sl, e_aq = ev(), ev(), ev(), ev()
    V.tensor_scalar(T.ident[:], T.mi[:], 4.0, T.pi[:, 0:1], AluOpType.mult, AluOpType.is_equal).then_inc(e_id, 1)
    V.wait_ge(e_s, 128)
    V.tensor_copy(T.s16[:], T.s32[:]).then_inc(e_s16, 1)
    for a in range(4):
        for b in range(2):
            V.tensor_scalar(T.sl[:, 16 * a + 8 * b:16 * a + 8 * b + 8], T.s32[:, 8 * a:8 * a + 8], float(b * W), None,
                            AluOpType.add).then_inc(e_sl, 1)
    V.wait_ge(e_a, 16)
    V.quantize_mx(T.aq[:], T.ap[:], T.at[:]).then_inc(e_aq, 1)

    PW = 2 * CAPP
    pairs = sorted(range(N // 2), key=lambda k: OWNAT if k == r // 2 else batch_of(2 * k, r))
    P.wait_ge(e_eq, 1)
    for c, k in enumerate(pairs):
        need = 0
        for s in (2 * k, 2 * k + 1):
            if s != r:
                need += 2 * len(lanes(topo, cores, s, batches(topo, cores, s)[batch_of(s, r)])[r])
        if k == r // 2:
            P.wait_ge(e_own, 32)
        P.wait_ge(T.sem["arr%d" % k], need)
        for o in UORD:
            e_u, e_d = ev(), T.sem["dw%d" % o]
            if c:
                P.wait_ge(e_d, c)
            P.matmul_mx(T.psu[:, 512 * o:512 * o + PW], T.eq[:, 128 * o:128 * o + 128], T.ep[:, 128 * o:128 * o + 128],
                        T.cq[:, PW * k:PW * k + PW], T.cp[:, PW * k:PW * k + PW], True, True).then_inc(e_u, 1)
            q = V if o % 2 == 0 else A
            q.wait_ge(e_u, 1)
            copy(q, T.dw[:, W * o + PW * k:W * o + PW * k + PW], T.psu[:, 512 * o:512 * o + PW], e_d)

    e_gt = [ev() for _ in range(2)]
    e_gl = [ev() for _ in range(2)]
    e_gm = [ev() for _ in range(2)]
    e_t, e_h, e_hq, e_y, e_ye = ([ev() for _ in range(4)] for _ in range(5))
    e_out = ev()
    hs = S // 2
    for q in (V, A):
        q.wait_ge(e_s16, 1)
        q.wait_ge(e_sl, 8)

    def pick(o):
        for h, q in enumerate((V, A)):
            q.wait_ge(T.sem["dw%d" % o], 4)
            copy(q, T.gt[:, S * o + hs * h:S * o + hs * h + hs],
                 T.dw[:, W * o:W * o + W].indirect(T.s16[:, 16 * h:16 * h + 16]), e_gt[o])

    def pick_both():
        for h, q in enumerate((V, A)):
            q.wait_ge(T.sem.dw2, 4)
            q.wait_ge(T.sem.dw3, 4)
            copy(q, T.gl[:, S * h:S * h + S], T.dw[:, 2 * W:4 * W].indirect(T.sl[:, 32 * h:32 * h + 32]), e_gl[h])
        for k in range(2):
            for h in range(2):
                if k == 0:
                    Y.wait_ge(e_gl[h], 1)
                for a in (2 * h, 2 * h + 1):
                    for s in (2 * k, 2 * k + 1):
                        Y.dma_start(T.gm[32 * a:32 * a + 32, hs * s:hs * s + hs],
                                    T.gl[32 * s:32 * s + 32, hs * a:hs * a + hs]).then_inc(e_gm[k], 16)

    def turn(o):
        P.wait_ge(e_gt[o], 2)
        b = 512 * o
        for t in range(4):
            P.transpose(T.pst[:, b + t:b + 512:4], T.gt[:, b + t:b + 512:4], T.ident[:]).then_inc(e_t[o], 1)

    def turn_here(o):
        V.wait_ge(e_gm[o - 2], 128)
        b = S * (o - 2)
        for t in range(4):
            V.transpose(T.ht[:, 512 * o + t:512 * o + 512:4], T.gm[:, b + t:b + S:4]).then_inc(e_h[o], 1)

    def empty(o, q):
        q.wait_ge(e_t[o], 4)
        copy(q, T.ht[:, 512 * o:512 * o + 512], T.pst[:, 512 * o:512 * o + 512], e_h[o])

    def quant(o):
        n = 1 if o < 2 else 4
        V.wait_ge(e_h[o], n)
        V.quantize_mx(T.hq[:, 128 * o:128 * o + 128], T.hp[:, 128 * o:128 * o + 128],
                      T.ht[:, 512 * o:512 * o + 512]).then_inc(e_hq[o], 1)
        Y.wait_ge(e_h[o], n)
        Y.dma_start(T.h[:, 512 * o:512 * o + 512], T.ht[:, 512 * o:512 * o + 512]).then_inc(e_out, 16)

    bank = {}

    def product(o):
        n = len(bank)
        bank[o] = T.psy[:, 512 * n:512 * n + NA] if n < 2 else T.psu[:, 512 * (n - 2):512 * (n - 2) + NA]
        P.wait_ge(e_hq[o], 1)
        P.matmul_mx(bank[o], T.hq[:, 128 * o:128 * o + 128], T.hp[:, 128 * o:128 * o + 128], T.aq[:], T.ap[:],
                    True, True).then_inc(e_y[o], 1)

    def y_out(o, q):
        q.wait_ge(e_y[o], 1)
        copy(q, T.yt[:, NA * o:NA * o + NA], bank[o], e_ye[o])
        Y.wait_ge(e_ye[o], 1)
        Y.dma_start(T.y[:, NA * o:NA * o + NA], T.yt[:, NA * o:NA * o + NA]).then_inc(e_out, 16)

    P.wait_ge(e_id, 1)
    P.wait_ge(e_aq, 1)
    step = {"p": pick, "t": turn, "l": turn_here, "q": quant, "m": product, "e": empty, "y": y_out}
    for w in TAIL.split():
        if w == "L":
            pick_both()
        elif w[0] in "ey":
            step[w[0]](int(w[1]), V if w[2:] == "V" else A)
        else:
            step[w[0]](int(w[1]))
    Y.wait_ge(e_out, 128)
